import numpy as np
import ml_dtypes


def mxq(x, axis, fmt="e4m3"):
    dtype, down = {"e4m3": (ml_dtypes.float8_e4m3fn, 7), "e5m2": (ml_dtypes.float8_e5m2, 14)}[fmt]
    v = np.moveaxis(np.asarray(x, np.float32).astype(ml_dtypes.bfloat16).astype(np.float64), axis, -1)
    blocks = v.reshape(v.shape[:-1] + (-1, 32))
    amax = np.abs(blocks).max(-1, keepdims=True)
    byte = np.maximum(np.where(amax > 0, np.frexp(amax)[1] - 1 + 127, 0) - down, 1)
    scale = np.exp2(byte - 127.0)
    codes = (blocks / scale).astype(np.float32).astype(dtype).astype(np.float64)
    return np.moveaxis((codes * scale).reshape(v.shape), -1, axis)


WIDE = False


def mx_kscale(k):
    if not WIDE:
        return np.ones(k)
    levels = np.array([10, -10, 5, -5, 0])
    if k % 512:
        return np.exp2(np.random.permutation(np.resize(levels, k // 32))).repeat(32)
    a = np.empty((k // 512, 16))
    for p in range(k // 512):
        a[p, :8] = np.random.permutation(np.resize(levels, 8))
        for g in range(8):
            far = levels[np.abs(levels - a[p, g]) >= 10]
            a[p, g + 8] = far[np.random.randint(len(far))]
    return np.exp2(a.ravel()).repeat(32)


def f64(x):
    return np.asarray(x).astype(np.float64)


def striped(idx):
    return np.tile(idx.reshape(-1, 16).T, (8, 1)).astype(np.uint16)


def unstriped(offs):
    return offs[:16].T.reshape(-1).astype(np.int64)


def striped8(idx):
    return np.concatenate([x.reshape(-1, 16).T for x in idx]).astype(np.uint16)


def runs(offs, k):
    lists = np.stack([offs[16 * r : 16 * r + 16].T.reshape(-1) for r in range(8)]).astype(np.int64)
    return lists[np.arange(k) % 512 // 64]


def pack_weight(w):
    k, n = w.shape
    w = f64(np.asarray(w, np.float32).astype(ml_dtypes.bfloat16)).reshape(k // 32, 32, n)
    amax = np.abs(w).max(1)
    byte = np.clip(np.where(amax > 0, np.frexp(amax)[1] - 1 + 127 - 7, 1), 1, 254)
    scaled = (w * np.exp2(127.0 - byte)[:, None, :]).reshape(k, n).astype(np.float32)
    words = np.ascontiguousarray(scaled.reshape(k // 512, 128, 4, n).transpose(0, 1, 3, 2)).astype(ml_dtypes.float8_e4m3fn).view(np.uint8)
    return words, np.ascontiguousarray(byte.astype(np.uint8).reshape(k // 512, 16, n))


def unpack_weight(words, scales):
    g, p, n, _ = words.shape
    vals = np.ascontiguousarray(words).view(ml_dtypes.float8_e4m3fn).astype(np.float64) * np.repeat(np.exp2(scales.astype(np.float64) - 127.0), 8, axis=1)[..., None]
    return vals.transpose(0, 1, 3, 2).reshape(g * 512, n)


E2M1 = np.array([0.0, 0.5, 1.0, 1.5, 2.0, 3.0, 4.0, 6.0, -0.0, -0.5, -1.0, -1.5, -2.0, -3.0, -4.0, -6.0])


def pack_fp4(w):
    k, n = w.shape
    w = f64(np.asarray(w, np.float32).astype(ml_dtypes.bfloat16)).reshape(k // 32, 32, n)
    amax = np.abs(w).max(1)
    mant, ex = np.frexp(amax / 6.0)
    byte = np.clip(np.where(amax > 0, np.where(mant > 0.5, ex, ex - 1) + 127, 1), 1, 254)
    scaled = (w * np.exp2(127.0 - byte)[:, None, :]).reshape(k, n).astype(np.float32)
    c = np.ascontiguousarray(scaled.reshape(k // 512, 128, 4, n).transpose(0, 1, 3, 2)).astype(ml_dtypes.float4_e2m1fn).view(np.uint8) & 0xF
    words = (c[..., 0::2] | (c[..., 1::2] << 4)).reshape(k // 512, 128, 2 * n)
    return np.ascontiguousarray(words), np.ascontiguousarray(byte.astype(np.uint8).reshape(k // 512, 16, n))


def unpack_fp4(words, scales):
    g, _, n = scales.shape
    words = np.ascontiguousarray(words).reshape(g, 128, n, 2)
    nib = np.empty((g, 128, n, 4), np.uint8)
    nib[..., 0::2] = words & 0xF
    nib[..., 1::2] = words >> 4
    vals = E2M1[nib] * np.repeat(np.exp2(scales.astype(np.float64) - 127.0), 8, axis=1)[..., None]
    return vals.transpose(0, 1, 3, 2).reshape(g * 512, n)


K, T, S, H, W, G = 512, 1024, 256, 512, 128, 2048


def setup_inputs():
    n = np.random.standard_normal
    s = mx_kscale(K)[:, None]
    packed_xT = pack_weight(n((K, T)) * s)
    packed_w1 = pack_fp4(n((K, H)) / np.sqrt(K) / s)
    packed_dT = pack_weight(n((K, G)) / s)
    perm = np.random.permutation(S)
    perm2 = np.random.permutation(S)
    perm3 = np.random.permutation(S)
    return {
        "x_words": packed_xT[0],
        "x_scales": packed_xT[1],
        "w1_words": packed_w1[0],
        "w1_scales": packed_w1[1],
        "gs": (np.random.uniform(0.5, 1.5, (K, 1)) * s).astype(np.float32),
        "d_words": packed_dT[0],
        "d_scales": packed_dT[1],
        "offs": striped(np.random.permutation(T)[:S]),
        "n1": striped(perm[:W]),
        "n2": striped(perm[W:]),
        "n3": striped(perm2[:W]),
        "n4": striped(perm2[W:]),
        "n5": striped(np.random.permutation(S)),
        "k1": striped8(np.random.randint(0, G, (8, H))),
        "k2": striped8(np.random.randint(0, G, (8, H))),
        "two": striped(np.random.permutation(T)[:S]),
        "k3": striped8(np.random.randint(0, G, (8, H))),
        "hz": striped8(np.random.randint(0, T, (8, S))),
        "n6": striped(perm3[:W]),
        "n7": striped(perm3[W:]),
    }


def reference(x_words, x_scales, w1_words, w1_scales, gs, d_words, d_scales, offs, n1, n2, n3, n4, n5, k1, k2, two, k3, hz, n6, n7):
    d_k1 = unpack_weight(d_words, d_scales)[np.arange(K)[:, None], runs(k1, K)]
    xq = unpack_weight(x_words, x_scales)[:, unstriped(offs)]
    y = unpack_fp4(w1_words, w1_scales).T @ xq
    pa = y[:, unstriped(n1)]
    pb = y[:, unstriped(n2)]
    rb = pa + pb
    ra = np.minimum(pa, pb)
    ua = np.zeros((H, S))
    ua[:, unstriped(n3)] = ra
    ub = ua.copy()
    ub[:, unstriped(n4)] = rb
    ds = np.zeros((H, S))
    ds[:, unstriped(n5)] = ub
    z = f64(gs) * (ub - ds)
    d_k2 = unpack_weight(d_words, d_scales)[np.arange(K)[:, None], runs(k2, K)]
    x_two = unpack_weight(x_words, x_scales)[:, unstriped(two)]
    d_k3 = unpack_weight(d_words, d_scales)[np.arange(K)[:, None], runs(k3, K)]
    x_hz = unpack_weight(x_words, x_scales)[np.arange(K)[:, None], runs(hz, K)]
    h2 = 0.0625 * ((d_k1.T @ mxq(z, 0, "e4m3") + d_k2.T @ x_two + d_k3.T @ x_hz))
    pa2 = h2[:, unstriped(n6)]
    pb2 = h2[:, unstriped(n7)]
    rb2 = pa2 - pb2
    ra2 = 0.75 * (pa2 + pb2)
    ua2 = np.zeros((H, S))
    ua2[:, unstriped(n6)] = ra2
    out = ua2.copy()
    out[:, unstriped(n7)] = rb2
    return out

@@ -1,0 +1,191 @@
+from contextlib import ExitStack
+
+import concourse.mybir as mybir
+
+F32 = mybir.dt.float32
+BF16 = mybir.dt.bfloat16
+I32 = mybir.dt.int32
+U32 = mybir.dt.uint32
+U16 = mybir.dt.uint16
+U8 = mybir.dt.uint8
+FP8X4 = mybir.dt.float8_e4m3fn_x4
+FP4X4 = mybir.dt.float4_e2m1fn_x4
+ALU = mybir.AluOpType
+COPY = mybir.ActivationFunctionType.Copy
+
+P = 128
+PACK = 4
+T, S, H, W, G = 1024, 256, 512, 128, 2048
+FLOPS = 4 * 2 * 512 * H * S
+
+
+def tile_picked_dtzmthcpsdhaar_none_p_kernel(
+    tc, x_words, x_scales, w1_words, w1_scales, gs, d_words, d_scales,
+    offs, n1, n2, n3, n4, n5, k1, k2, two, k3, hz, n6, n7, out,
+):
+    nc = tc.nc
+    with ExitStack() as ctx:
+        lists = ctx.enter_context(tc.tile_pool(name="lists", bufs=1))
+        keep = ctx.enter_context(tc.tile_pool(name="keep", bufs=1))
+        psum = ctx.enter_context(tc.psum_pool(name="psum", bufs=1))
+
+        def load_list(name, src):
+            tile = lists.tile(list(src.shape), U16, name="list_" + name)
+            nc.sync.dma_start(tile[:], src)
+            return tile
+
+        def load_scales(queue, name, src, cols):
+            tile = keep.tile([P, cols], U8, name=name, align_bytes=64)
+            rows = src[0].bitcast(I32)
+            for q in range(4):
+                queue.dma_start(tile[32 * q:32 * q + 32, :].bitcast(I32), rows[4 * q:4 * q + 4, :].partition_broadcast(8))
+            return tile
+
+        def load_words(queue, name, src, cols, tag):
+            tile = keep.tile([P, cols], U32, name=name, tag=tag, align_bytes=64)
+            queue.dma_start(tile[:].bitcast(I32), src[0].rearrange("p n t -> p (n t)").bitcast(I32))
+            return tile
+
+        def gather(dst, window, offsets):
+            nc.vector.tensor_copy(dst, window[:].indirect(offsets[:]))
+
+        gain = keep.tile([P, PACK], F32, name="gain")
+        nc.gpsimd.dma_start(gain[:], gs.rearrange("(p t) o -> p (t o)", t=PACK))
+        xs = load_scales(nc.scalar, "xs", x_scales, T)
+        l_offs = load_list("offs", offs)
+        xw = load_words(nc.sync, "xw", x_words, T, "xw")
+        w1s = load_scales(nc.sync, "w1s", w1_scales, H)
+        w1w = keep.tile([P, 2 * H], U8, name="w1w", align_bytes=64)
+        nc.sync.dma_start(w1w[:].bitcast(I32), w1_words[0].bitcast(I32))
+        neg_gain = keep.tile([P, PACK], F32, name="neg_gain")
+        nc.scalar.activation(neg_gain[:], gain[:], COPY, scale=-1.0)
+        l_n1 = load_list("n1", n1)
+        l_n2 = load_list("n2", n2)
+        l_n3 = load_list("n3", n3)
+        l_n4 = load_list("n4", n4)
+        ds_ = keep.tile([P, G], U8, name="dsc", align_bytes=64)
+        nc.gpsimd.memset(ds_[:].bitcast(I32), 0)
+        for r in range(4):
+            first = r if r < 2 else 16 + r
+            nc.sync.dma_start(ds_[first:P:32, :].bitcast(I32), d_scales[0].bitcast(I32)[r:16:4, :])
+        l_k1 = load_list("k1", k1)
+        l_k2 = load_list("k2", k2)
+        l_k3 = load_list("k3", k3)
+        l_hz = load_list("hz", hz)
+        l_two = load_list("two", two)
+        dw = load_words(nc.sync, "dw", d_words, G, "dw_then_z")
+        l_n5 = load_list("n5", n5)
+        l_n6 = load_list("n6", n6)
+        l_n7 = load_list("n7", n7)
+
+        xq_s = keep.tile([P, S], U8, name="xq_s", align_bytes=64)
+        gather(xq_s[:], xs, l_offs)
+        w_codes, w_scales = [], []
+        for t in range(PACK):
+            wc = keep.tile([P, 2 * P], U8, name="wc%d" % t, align_bytes=64)
+            nc.scalar.copy(wc[:].bitcast(U16), w1w[:].bitcast(U16)[:, t::PACK])
+            w_codes.append(wc)
+            w_scales.append(keep.tile([P, P], U8, name="ws%d" % t, align_bytes=64))
+        nc.vector.tensor_copy(w_scales[0][:], w1s[:, 0::PACK])
+        xq_w = keep.tile([P, S], U32, name="xq_w", align_bytes=64)
+        gather(xq_w[:], xw, l_offs)
+        for t in range(1, PACK):
+            nc.vector.tensor_copy(w_scales[t][:], w1s[:, t::PACK])
+
+        y = []
+        for t in range(PACK):
+            bank = psum.tile([P, S], F32, name="ybank%d" % t)
+            nc.tensor.matmul_mx(
+                out=bank[:], lhsT=w_codes[t][:].bitcast(FP4X4), lhsT_scale=w_scales[t][:],
+                rhs=xq_w[:].bitcast(FP8X4), rhs_scale=xq_s[:], start=True, stop=True,
+            )
+            yt = keep.tile([P, S], F32, name="y%d" % t)
+            nc.vector.tensor_copy(yt[:], bank[:])
+            y.append(yt)
+
+        pairs, res = [], []
+        for t in range(PACK):
+            pr = keep.tile([P, 2, W], F32, name="pairs%d" % t)
+            nc.scalar.activation(pr[:, 0, :], y[t][:].indirect(l_n1[:]), COPY)
+            nc.scalar.activation(pr[:, 1, :], y[t][:].indirect(l_n2[:]), COPY)
+            pairs.append(pr)
+        for t in range(PACK):
+            r = keep.tile([P, 2, W], F32, name="res%d" % t)
+            nc.vector.tensor_tensor(r[:, 0, :], pairs[t][:, 0, :], pairs[t][:, 1, :], ALU.min)
+            nc.vector.tensor_tensor(r[:, 1, :], pairs[t][:, 0, :], pairs[t][:, 1, :], ALU.add)
+            res.append(r)
+        ub = [keep.tile([P, S], F32, name="ub%d" % t) for t in range(PACK)]
+        sent = [keep.tile([P, 2 * S], F32, name="sent%d" % t) for t in range(PACK)]
+        for t in range(PACK):
+            nc.scalar.activation(ub[t][:].indirect(l_n3[:]), res[t][:, 0, :], COPY)
+        for t in range(PACK):
+            nc.scalar.activation(ub[t][:].indirect(l_n4[:]), res[t][:, 1, :], COPY)
+        for t in range(PACK):
+            nc.scalar.activation(sent[t][:].indirect(l_n5[:]), ub[t][:], COPY)
+
+        picked = keep.tile([P, 3 * H + S], U8, name="picked", align_bytes=64)
+        for i, lst in enumerate((l_k1, l_k2, l_k3)):
+            gather(picked[:, i * H:(i + 1) * H], ds_, lst)
+        gather(picked[:, 3 * H:], xs, l_hz)
+        placed = keep.tile([P, 3 * H + S], U8, name="placed", align_bytes=64)
+        nc.vector.tensor_copy(placed[:].bitcast(I32), picked[:].bitcast(I32))
+        for r in (2, 3):
+            nc.sync.dma_start(placed[r:P:32, :].bitcast(I32), picked[16 + r:P:32, :].bitcast(I32))
+        two_s = keep.tile([P, S], U8, name="two_s", align_bytes=64)
+        gather(two_s[:], xs, l_two)
+        two_w = keep.tile([P, S], U32, name="two_w", align_bytes=64)
+        gather(two_w[:], xw, l_two)
+        hz_w = keep.tile([P, S], U32, name="hz_w", align_bytes=64)
+        gather(hz_w[:], xw, l_hz)
+        dk = []
+        for i, lst in enumerate((l_k1, l_k2, l_k3)):
+            tile = keep.tile([P, H], U32, name="dk%d" % i, align_bytes=64)
+            gather(tile[:], dw, lst)
+            dk.append(tile)
+
+        hbank = [psum.tile([P, S], F32, name="hbank%d" % b) for b in range(4)]
+
+        def product(b, i, rhs, rhs_scale, start, stop):
+            nc.tensor.matmul_mx(
+                out=hbank[b][:], lhsT=dk[i][:, b * P:(b + 1) * P].bitcast(FP8X4),
+                lhsT_scale=placed[:, i * H + b * P:i * H + (b + 1) * P],
+                rhs=rhs.bitcast(FP8X4), rhs_scale=rhs_scale, start=start, stop=stop,
+            )
+
+        for b in range(4):
+            product(b, 1, two_w[:], two_s[:], True, False)
+            product(b, 2, hz_w[:], placed[:, 3 * H:], False, False)
+
+        z = keep.tile([P, S, PACK], BF16, name="z", tag="dw_then_z", align_bytes=64)
+        for t in range(PACK):
+            ubg = keep.tile([P, S], F32, name="ubg%d" % t)
+            nc.vector.tensor_scalar(ubg[:], ub[t][:], gain[:, t:t + 1], None, ALU.mult)
+            nc.vector.scalar_tensor_tensor(
+                z[:, :, t], sent[t][:, 0:S], neg_gain[:, t:t + 1], ubg[:], ALU.mult, ALU.add)
+        z_w = keep.tile([P, S], U32, name="z_w", align_bytes=64)
+        z_s = keep.tile([P, S], U8, name="z_s", align_bytes=64)
+        nc.vector.quantize_mx(out=z_w[:].bitcast(FP8X4), scales=z_s[:], in_=z[:].rearrange("p j t -> p (j t)"))
+
+        h2 = []
+        for b in range(4):
+            product(b, 0, z_w[:], z_s[:], False, True)
+            hb = keep.tile([P, S], F32, name="h2_%d" % b)
+            nc.vector.tensor_scalar(hb[:], hbank[b][:], 0.0625, None, ALU.mult)
+            h2.append(hb)
+        pairs2, res2 = [], []
+        for b in range(4):
+            pr = keep.tile([P, 2, W], F32, name="pairs2_%d" % b)
+            nc.scalar.activation(pr[:, 0, :], h2[b][:].indirect(l_n6[:]), COPY)
+            nc.scalar.activation(pr[:, 1, :], h2[b][:].indirect(l_n7[:]), COPY)
+            pairs2.append(pr)
+        for b in range(4):
+            r = keep.tile([P, 2, W], F32, name="res2_%d" % b)
+            nc.vector.tensor_tensor(r[:, 0, :], pairs2[b][:, 0, :], pairs2[b][:, 1, :], ALU.add)
+            nc.vector.tensor_tensor(r[:, 1, :], pairs2[b][:, 0, :], pairs2[b][:, 1, :], ALU.subtract)
+            res2.append(r)
+        final = [keep.tile([P, S], F32, name="final%d" % b) for b in range(4)]
+        for b in range(4):
+            nc.scalar.activation(final[b][:].indirect(l_n6[:]), res2[b][:, 0, :], COPY, scale=0.75)
+        for b in range(4):
+            nc.scalar.activation(final[b][:].indirect(l_n7[:]), res2[b][:, 1, :], COPY)
+            nc.sync.dma_start(out[b * P:(b + 1) * P, :], final[b][:])

@@ -29,93 +29,91 @@ def tile_picked_dtzmthcpsdhaar_none_p_kernel(
         keep = ctx.enter_context(tc.tile_pool(name="keep", bufs=1))
         psum = ctx.enter_context(tc.psum_pool(name="psum", bufs=1))
 
+        def sb(name, shape, dtype, tag=None):
+            return keep.tile(shape, dtype, name=name, tag=tag or name, align_bytes=64)
+
         def load_list(name, src):
             tile = lists.tile(list(src.shape), U16, name="list_" + name)
             nc.sync.dma_start(tile[:], src)
             return tile
 
-        def load_scales(queue, name, src, cols):
-            tile = keep.tile([P, cols], U8, name=name, align_bytes=64)
-            rows = src[0].bitcast(I32)
-            for q in range(4):
-                queue.dma_start(tile[32 * q:32 * q + 32, :].bitcast(I32), rows[4 * q:4 * q + 4, :].partition_broadcast(8))
-            return tile
+        def load_quadrant(queue, tile, src, q):
+            rows = src[0].bitcast(I32)[4 * q:4 * q + 4, :]
+            queue.dma_start(tile[32 * q:32 * q + 32, :].bitcast(I32), rows.partition_broadcast(8))
 
-        def load_words(queue, name, src, cols, tag):
-            tile = keep.tile([P, cols], U32, name=name, tag=tag, align_bytes=64)
+        def load_words(queue, name, src, cols):
+            tile = sb(name, [P, cols], U32)
             queue.dma_start(tile[:].bitcast(I32), src[0].rearrange("p n t -> p (n t)").bitcast(I32))
             return tile
 
         def gather(dst, window, offsets):
             nc.vector.tensor_copy(dst, window[:].indirect(offsets[:]))
 
-        gain = keep.tile([P, PACK], F32, name="gain")
-        nc.gpsimd.dma_start(gain[:], gs.rearrange("(p t) o -> p (t o)", t=PACK))
-        xs = load_scales(nc.scalar, "xs", x_scales, T)
+        xs = sb("xs", [P, T], U8)
+        w1s = sb("w1s", [P, H], U8)
+        load_quadrant(nc.gpsimd, w1s, w1_scales, 3)
+        load_quadrant(nc.scalar, xs, x_scales, 0)
+        load_quadrant(nc.sync, xs, x_scales, 3)
+        load_quadrant(nc.scalar, xs, x_scales, 1)
+        load_quadrant(nc.sync, xs, x_scales, 2)
+        load_quadrant(nc.scalar, w1s, w1_scales, 0)
         l_offs = load_list("offs", offs)
-        xw = load_words(nc.sync, "xw", x_words, T, "xw")
-        w1s = load_scales(nc.sync, "w1s", w1_scales, H)
-        w1w = keep.tile([P, 2 * H], U8, name="w1w", align_bytes=64)
-        nc.sync.dma_start(w1w[:].bitcast(I32), w1_words[0].bitcast(I32))
-        neg_gain = keep.tile([P, PACK], F32, name="neg_gain")
-        nc.scalar.activation(neg_gain[:], gain[:], COPY, scale=-1.0)
+        xw = load_words(nc.sync, "xw", x_words, T)
+        w1w = sb("w1w", [P, 2 * H], U8)
+        nc.scalar.dma_start(w1w[:].bitcast(I32), w1_words[0].bitcast(I32))
+        load_quadrant(nc.sync, w1s, w1_scales, 1)
+        load_quadrant(nc.sync, w1s, w1_scales, 2)
         l_n1 = load_list("n1", n1)
         l_n2 = load_list("n2", n2)
         l_n3 = load_list("n3", n3)
         l_n4 = load_list("n4", n4)
-        ds_ = keep.tile([P, G], U8, name="dsc", align_bytes=64)
-        nc.gpsimd.memset(ds_[:].bitcast(I32), 0)
+        dsc = sb("dsc", [P, G], U8)
+        nc.vector.memset(dsc[:].bitcast(I32), 0)
         for r in range(4):
             first = r if r < 2 else 16 + r
-            nc.sync.dma_start(ds_[first:P:32, :].bitcast(I32), d_scales[0].bitcast(I32)[r:16:4, :])
+            nc.sync.dma_start(dsc[first:P:32, :].bitcast(I32), d_scales[0].bitcast(I32)[r:16:4, :])
         l_k1 = load_list("k1", k1)
         l_k2 = load_list("k2", k2)
         l_k3 = load_list("k3", k3)
         l_hz = load_list("hz", hz)
         l_two = load_list("two", two)
-        dw = load_words(nc.sync, "dw", d_words, G, "dw_then_z")
+        dw = load_words(nc.sync, "dw", d_words, G)
         l_n5 = load_list("n5", n5)
+        gain = sb("gain", [P, PACK], F32)
+        nc.sync.dma_start(gain[:], gs.rearrange("(p t) o -> p (t o)", t=PACK))
         l_n6 = load_list("n6", n6)
         l_n7 = load_list("n7", n7)
 
-        xq_s = keep.tile([P, S], U8, name="xq_s", align_bytes=64)
+        xq_s = sb("xq_s", [P, S], U8)
         gather(xq_s[:], xs, l_offs)
-        w_codes, w_scales = [], []
-        for t in range(PACK):
-            wc = keep.tile([P, 2 * P], U8, name="wc%d" % t, align_bytes=64)
-            nc.scalar.copy(wc[:].bitcast(U16), w1w[:].bitcast(U16)[:, t::PACK])
-            w_codes.append(wc)
-            w_scales.append(keep.tile([P, P], U8, name="ws%d" % t, align_bytes=64))
-        nc.vector.tensor_copy(w_scales[0][:], w1s[:, 0::PACK])
-        xq_w = keep.tile([P, S], U32, name="xq_w", align_bytes=64)
+        xq_w = sb("xq_w", [P, S], U32)
         gather(xq_w[:], xw, l_offs)
-        for t in range(1, PACK):
-            nc.vector.tensor_copy(w_scales[t][:], w1s[:, t::PACK])
-
         y = []
         for t in range(PACK):
-            bank = psum.tile([P, S], F32, name="ybank%d" % t)
+            wc = sb("wc%d" % t, [P, 2 * P], U8)
+            nc.scalar.copy(wc[:].bitcast(U16), w1w[:].bitcast(U16)[:, t::PACK])
+            ws = sb("ws%d" % t, [P, P], U8)
+            nc.gpsimd.tensor_copy(ws[:], w1s[:, t::PACK])
+            bank = psum.tile([P, S], F32, name="ybank%d" % t, tag="bank%d" % t)
             nc.tensor.matmul_mx(
-                out=bank[:], lhsT=w_codes[t][:].bitcast(FP4X4), lhsT_scale=w_scales[t][:],
+                out=bank[:], lhsT=wc[:].bitcast(FP4X4), lhsT_scale=ws[:],
                 rhs=xq_w[:].bitcast(FP8X4), rhs_scale=xq_s[:], start=True, stop=True,
             )
-            yt = keep.tile([P, S], F32, name="y%d" % t)
+            yt = sb("y%d" % t, [P, S], F32)
             nc.vector.tensor_copy(yt[:], bank[:])
             y.append(yt)
 
-        pairs, res = [], []
+        pa = [sb("pa%d" % t, [P, W], F32) for t in range(PACK)]
+        pb = [sb("pb%d" % t, [P, W], F32) for t in range(PACK)]
+        res = [sb("res%d" % t, [P, 2, W], F32) for t in range(PACK)]
         for t in range(PACK):
-            pr = keep.tile([P, 2, W], F32, name="pairs%d" % t)
-            nc.scalar.activation(pr[:, 0, :], y[t][:].indirect(l_n1[:]), COPY)
-            nc.scalar.activation(pr[:, 1, :], y[t][:].indirect(l_n2[:]), COPY)
-            pairs.append(pr)
+            nc.scalar.activation(pa[t][:], y[t][:].indirect(l_n1[:]), COPY)
+            nc.scalar.activation(pb[t][:], y[t][:].indirect(l_n2[:]), COPY)
         for t in range(PACK):
-            r = keep.tile([P, 2, W], F32, name="res%d" % t)
-            nc.vector.tensor_tensor(r[:, 0, :], pairs[t][:, 0, :], pairs[t][:, 1, :], ALU.min)
-            nc.vector.tensor_tensor(r[:, 1, :], pairs[t][:, 0, :], pairs[t][:, 1, :], ALU.add)
-            res.append(r)
-        ub = [keep.tile([P, S], F32, name="ub%d" % t) for t in range(PACK)]
-        sent = [keep.tile([P, 2 * S], F32, name="sent%d" % t) for t in range(PACK)]
+            nc.vector.tensor_tensor(res[t][:, 0, :], pa[t][:], pb[t][:], ALU.min)
+            nc.vector.tensor_tensor(res[t][:, 1, :], pa[t][:], pb[t][:], ALU.add)
+        ub = [sb("ub%d" % t, [P, S], F32) for t in range(PACK)]
+        sent = [sb("sent%d" % t, [P, 2 * S], F32) for t in range(PACK)]
         for t in range(PACK):
             nc.scalar.activation(ub[t][:].indirect(l_n3[:]), res[t][:, 0, :], COPY)
         for t in range(PACK):
@@ -123,67 +121,71 @@ def tile_picked_dtzmthcpsdhaar_none_p_kernel(
         for t in range(PACK):
             nc.scalar.activation(sent[t][:].indirect(l_n5[:]), ub[t][:], COPY)
 
-        picked = keep.tile([P, 3 * H + S], U8, name="picked", align_bytes=64)
+        picked = sb("picked", [P, 3 * H + 2 * S], U8, tag="pa3")
+        words = sb("words", [P, 3 * H + 2 * S], U32, tag="pb3")
+        moved = 3 * H + S
         for i, lst in enumerate((l_k1, l_k2, l_k3)):
-            gather(picked[:, i * H:(i + 1) * H], ds_, lst)
-        gather(picked[:, 3 * H:], xs, l_hz)
-        placed = keep.tile([P, 3 * H + S], U8, name="placed", align_bytes=64)
-        nc.vector.tensor_copy(placed[:].bitcast(I32), picked[:].bitcast(I32))
+            gather(picked[:, i * H:(i + 1) * H], dsc, lst)
+        gather(picked[:, 3 * H:moved], xs, l_hz)
+        placed = sb("placed", [P, moved], U8)
+        nc.vector.tensor_copy(placed[:].bitcast(I32), picked[:, 0:moved].bitcast(I32))
         for r in (2, 3):
-            nc.sync.dma_start(placed[r:P:32, :].bitcast(I32), picked[16 + r:P:32, :].bitcast(I32))
-        two_s = keep.tile([P, S], U8, name="two_s", align_bytes=64)
-        gather(two_s[:], xs, l_two)
-        two_w = keep.tile([P, S], U32, name="two_w", align_bytes=64)
-        gather(two_w[:], xw, l_two)
-        hz_w = keep.tile([P, S], U32, name="hz_w", align_bytes=64)
-        gather(hz_w[:], xw, l_hz)
-        dk = []
-        for i, lst in enumerate((l_k1, l_k2, l_k3)):
-            tile = keep.tile([P, H], U32, name="dk%d" % i, align_bytes=64)
-            gather(tile[:], dw, lst)
-            dk.append(tile)
+            nc.sync.dma_start(placed[r:P:32, :].bitcast(I32), picked[16 + r:P:32, 0:moved].bitcast(I32))
+        gather(picked[:, moved:], xs, l_two)
+        gather(words[:, 3 * H:moved], xw, l_hz)
+        gather(words[:, moved:], xw, l_two)
+        for i, lst in ((1, l_k2), (2, l_k3), (0, l_k1)):
+            gather(words[:, i * H:(i + 1) * H], dw, lst)
 
-        hbank = [psum.tile([P, S], F32, name="hbank%d" % b) for b in range(4)]
+        groups = [(0, 0, W), (0, W, W)] + [(b, 0, S) for b in range(1, 4)]
+        hbank = [psum.tile([P, n], F32, name="hbank%d" % g, tag="bank%d" % (7 - g)) for g, (b, c, n) in enumerate(groups)]
 
-        def product(b, i, rhs, rhs_scale, start, stop):
+        def product(g, i, rhs, rhs_scale, start, stop):
+            b, c, n = groups[g]
+            cols = slice(i * H + b * P, i * H + (b + 1) * P)
             nc.tensor.matmul_mx(
-                out=hbank[b][:], lhsT=dk[i][:, b * P:(b + 1) * P].bitcast(FP8X4),
-                lhsT_scale=placed[:, i * H + b * P:i * H + (b + 1) * P],
-                rhs=rhs.bitcast(FP8X4), rhs_scale=rhs_scale, start=start, stop=stop,
+                out=hbank[g][:], lhsT=words[:, cols].bitcast(FP8X4), lhsT_scale=placed[:, cols],
+                rhs=rhs[:, c:c + n].bitcast(FP8X4), rhs_scale=rhs_scale[:, c:c + n], start=start, stop=stop,
             )
 
-        for b in range(4):
-            product(b, 1, two_w[:], two_s[:], True, False)
-            product(b, 2, hz_w[:], placed[:, 3 * H:], False, False)
+        for g in range(len(groups)):
+            product(g, 1, words[:, moved:], picked[:, moved:], True, False)
+            product(g, 2, words[:, 3 * H:moved], placed[:, 3 * H:], False, False)
 
-        z = keep.tile([P, S, PACK], BF16, name="z", tag="dw_then_z", align_bytes=64)
+        neg_gain = sb("neg_gain", [P, PACK], F32)
+        nc.vector.tensor_scalar(neg_gain[:], gain[:], -1.0, None, ALU.mult)
+        z = sb("z", [P, S, PACK], BF16, tag="dw")
         for t in range(PACK):
-            ubg = keep.tile([P, S], F32, name="ubg%d" % t)
+            ubg = sb("ubg%d" % t, [P, S], F32, tag="dsc" if t == 0 else None)
             nc.vector.tensor_scalar(ubg[:], ub[t][:], gain[:, t:t + 1], None, ALU.mult)
-            nc.vector.scalar_tensor_tensor(
-                z[:, :, t], sent[t][:, 0:S], neg_gain[:, t:t + 1], ubg[:], ALU.mult, ALU.add)
-        z_w = keep.tile([P, S], U32, name="z_w", align_bytes=64)
-        z_s = keep.tile([P, S], U8, name="z_s", align_bytes=64)
-        nc.vector.quantize_mx(out=z_w[:].bitcast(FP8X4), scales=z_s[:], in_=z[:].rearrange("p j t -> p (j t)"))
+            pieces = 2 if t == PACK - 1 else 1
+            for c in range(pieces):
+                cols = slice(c * S // pieces, (c + 1) * S // pieces)
+                nc.vector.scalar_tensor_tensor(
+                    z[:, cols, t], sent[t][:, cols], neg_gain[:, t:t + 1], ubg[:, cols], ALU.mult, ALU.add)
+        z_w = sb("z_w", [P, S], U32)
+        z_s = sb("z_s", [P, S], U8)
+        for c in range(2):
+            cols = slice(c * W, (c + 1) * W)
+            nc.vector.quantize_mx(
+                out=z_w[:, cols].bitcast(FP8X4), scales=z_s[:, cols], in_=z[:, cols, :].rearrange("p j t -> p (j t)"))
 
-        h2 = []
+        h2 = [sb("h2_%d" % b, [P, S], F32) for b in range(4)]
+        for g, (b, c, n) in enumerate(groups):
+            product(g, 0, z_w[:], z_s[:], False, True)
+            if g == 0:
+                nc.scalar.activation(h2[b][:, c:c + n], hbank[g][:], COPY, scale=0.0625)
+            else:
+                nc.vector.tensor_scalar(h2[b][:, c:c + n], hbank[g][:], 0.0625, None, ALU.mult)
+        pairs2 = [sb("pairs2_%d" % b, [P, 2, W], F32) for b in range(4)]
+        res2 = [sb("res2_%d" % b, [P, 2, W], F32) for b in range(4)]
         for b in range(4):
-            product(b, 0, z_w[:], z_s[:], False, True)
-            hb = keep.tile([P, S], F32, name="h2_%d" % b)
-            nc.vector.tensor_scalar(hb[:], hbank[b][:], 0.0625, None, ALU.mult)
-            h2.append(hb)
-        pairs2, res2 = [], []
+            nc.scalar.activation(pairs2[b][:, 0, :], h2[b][:].indirect(l_n6[:]), COPY)
+            nc.scalar.activation(pairs2[b][:, 1, :], h2[b][:].indirect(l_n7[:]), COPY)
         for b in range(4):
-            pr = keep.tile([P, 2, W], F32, name="pairs2_%d" % b)
-            nc.scalar.activation(pr[:, 0, :], h2[b][:].indirect(l_n6[:]), COPY)
-            nc.scalar.activation(pr[:, 1, :], h2[b][:].indirect(l_n7[:]), COPY)
-            pairs2.append(pr)
-        for b in range(4):
-            r = keep.tile([P, 2, W], F32, name="res2_%d" % b)
-            nc.vector.tensor_tensor(r[:, 0, :], pairs2[b][:, 0, :], pairs2[b][:, 1, :], ALU.add)
-            nc.vector.tensor_tensor(r[:, 1, :], pairs2[b][:, 0, :], pairs2[b][:, 1, :], ALU.subtract)
-            res2.append(r)
-        final = [keep.tile([P, S], F32, name="final%d" % b) for b in range(4)]
+            nc.vector.tensor_tensor(res2[b][:, 0, :], pairs2[b][:, 0, :], pairs2[b][:, 1, :], ALU.add)
+            nc.vector.tensor_tensor(res2[b][:, 1, :], pairs2[b][:, 0, :], pairs2[b][:, 1, :], ALU.subtract)
+        final = [sb("final%d" % b, [P, S], F32) for b in range(4)]
         for b in range(4):
             nc.scalar.activation(final[b][:].indirect(l_n6[:]), res2[b][:, 0, :], COPY, scale=0.75)
         for b in range(4):

@@ -87,21 +87,25 @@ def tile_picked_dtzmthcpsdhaar_none_p_kernel(
         xq_s = sb("xq_s", [P, S], U8)
         gather(xq_s[:], xs, l_offs)
         xq_w = sb("xq_w", [P, S], U32)
-        gather(xq_w[:], xw, l_offs)
-        y = []
+        for c in range(2):
+            nc.vector.tensor_copy(xq_w[:, c * W:(c + 1) * W], xw[:].indirect(l_offs[:, c * W // 16:(c + 1) * W // 16]))
+        groups = [(0, 0, W), (0, W, W)] + [(b, 0, S) for b in range(1, 4)]
+        wc = [sb("wc%d" % t, [P, 2 * P], U8) for t in range(PACK)]
+        ws = [sb("ws%d" % t, [P, P], U8) for t in range(PACK)]
         for t in range(PACK):
-            wc = sb("wc%d" % t, [P, 2 * P], U8)
-            nc.scalar.copy(wc[:].bitcast(U16), w1w[:].bitcast(U16)[:, t::PACK])
-            ws = sb("ws%d" % t, [P, P], U8)
-            nc.gpsimd.tensor_copy(ws[:], w1s[:, t::PACK])
-            bank = psum.tile([P, S], F32, name="ybank%d" % t, tag="bank%d" % t)
+            nc.scalar.copy(wc[t][:].bitcast(U16), w1w[:].bitcast(U16)[:, t::PACK])
+            nc.gpsimd.tensor_copy(ws[t][:], w1s[:, t::PACK])
+        y = [sb("y%d" % t, [P, S], F32) for t in range(PACK)]
+        for g, (t, c, n) in enumerate(groups):
+            bank = psum.tile([P, n], F32, name="ybank%d" % g, tag="bank%d" % g)
             nc.tensor.matmul_mx(
-                out=bank[:], lhsT=wc[:].bitcast(FP4X4), lhsT_scale=ws[:],
-                rhs=xq_w[:].bitcast(FP8X4), rhs_scale=xq_s[:], start=True, stop=True,
+                out=bank[:], lhsT=wc[t][:].bitcast(FP4X4), lhsT_scale=ws[t][:],
+                rhs=xq_w[:, c:c + n].bitcast(FP8X4), rhs_scale=xq_s[:, c:c + n], start=True, stop=True,
             )
-            yt = sb("y%d" % t, [P, S], F32)
-            nc.vector.tensor_copy(yt[:], bank[:])
-            y.append(yt)
+            if g == 0:
+                nc.scalar.copy(y[t][:, c:c + n], bank[:])
+            else:
+                nc.vector.tensor_copy(y[t][:, c:c + n], bank[:])
 
         pa = [sb("pa%d" % t, [P, W], F32) for t in range(PACK)]
         pb = [sb("pb%d" % t, [P, W], F32) for t in range(PACK)]
@@ -114,30 +118,30 @@ def tile_picked_dtzmthcpsdhaar_none_p_kernel(
             nc.vector.tensor_tensor(res[t][:, 1, :], pa[t][:], pb[t][:], ALU.add)
         ub = [sb("ub%d" % t, [P, S], F32) for t in range(PACK)]
         sent = [sb("sent%d" % t, [P, 2 * S], F32) for t in range(PACK)]
-        for t in range(PACK):
-            nc.scalar.activation(ub[t][:].indirect(l_n3[:]), res[t][:, 0, :], COPY)
-        for t in range(PACK):
-            nc.scalar.activation(ub[t][:].indirect(l_n4[:]), res[t][:, 1, :], COPY)
+        for first in (0, 2):
+            for lst, side in ((l_n3, 0), (l_n4, 1)):
+                for t in (first, first + 1):
+                    nc.scalar.activation(ub[t][:].indirect(lst[:]), res[t][:, side, :], COPY)
         for t in range(PACK):
             nc.scalar.activation(sent[t][:].indirect(l_n5[:]), ub[t][:], COPY)
 
-        picked = sb("picked", [P, 3 * H + 2 * S], U8, tag="pa3")
+        picked = sb("picked", [P, 3 * H + 2 * S], U8, tag="pa1")
         words = sb("words", [P, 3 * H + 2 * S], U32, tag="pb3")
         moved = 3 * H + S
         for i, lst in enumerate((l_k1, l_k2, l_k3)):
             gather(picked[:, i * H:(i + 1) * H], dsc, lst)
         gather(picked[:, 3 * H:moved], xs, l_hz)
         placed = sb("placed", [P, moved], U8)
-        nc.vector.tensor_copy(placed[:].bitcast(I32), picked[:, 0:moved].bitcast(I32))
-        for r in (2, 3):
-            nc.sync.dma_start(placed[r:P:32, :].bitcast(I32), picked[16 + r:P:32, 0:moved].bitcast(I32))
+        nc.gpsimd.memset(placed[:].bitcast(I32), 0)
+        for r in range(4):
+            first = r if r < 2 else 16 + r
+            nc.sync.dma_start(placed[r:P:32, :].bitcast(I32), picked[first:P:32, 0:moved].bitcast(I32))
         gather(picked[:, moved:], xs, l_two)
         gather(words[:, 3 * H:moved], xw, l_hz)
         gather(words[:, moved:], xw, l_two)
         for i, lst in ((1, l_k2), (2, l_k3), (0, l_k1)):
             gather(words[:, i * H:(i + 1) * H], dw, lst)
 
-        groups = [(0, 0, W), (0, W, W)] + [(b, 0, S) for b in range(1, 4)]
         hbank = [psum.tile([P, n], F32, name="hbank%d" % g, tag="bank%d" % (7 - g)) for g, (b, c, n) in enumerate(groups)]
 
         def product(g, i, rhs, rhs_scale, start, stop):
@@ -152,17 +156,20 @@ def tile_picked_dtzmthcpsdhaar_none_p_kernel(
             product(g, 1, words[:, moved:], picked[:, moved:], True, False)
             product(g, 2, words[:, 3 * H:moved], placed[:, 3 * H:], False, False)
 
-        neg_gain = sb("neg_gain", [P, PACK], F32)
-        nc.vector.tensor_scalar(neg_gain[:], gain[:], -1.0, None, ALU.mult)
         z = sb("z", [P, S, PACK], BF16, tag="dw")
-        for t in range(PACK):
-            ubg = sb("ubg%d" % t, [P, S], F32, tag="dsc" if t == 0 else None)
-            nc.vector.tensor_scalar(ubg[:], ub[t][:], gain[:, t:t + 1], None, ALU.mult)
-            pieces = 2 if t == PACK - 1 else 1
-            for c in range(pieces):
-                cols = slice(c * S // pieces, (c + 1) * S // pieces)
-                nc.vector.scalar_tensor_tensor(
-                    z[:, cols, t], sent[t][:, cols], neg_gain[:, t:t + 1], ubg[:, cols], ALU.mult, ALU.add)
+        last = PACK - 1
+        for t in range(last):
+            diff = sb("diff%d" % t, [P, S], F32, tag="dsc" if t == 0 else None)
+            nc.vector.tensor_tensor(diff[:], ub[t][:], sent[t][:, 0:S], ALU.subtract)
+            nc.vector.tensor_scalar(z[:, :, t], diff[:], gain[:, t:t + 1], None, ALU.mult)
+        neg_gain = sb("neg_gain", [P, 1], F32)
+        nc.vector.tensor_scalar(neg_gain[:], gain[:, last:], -1.0, None, ALU.mult)
+        ub_gain = sb("ub_gain", [P, S], F32, tag="xw")
+        nc.vector.tensor_scalar(ub_gain[:], ub[last][:], gain[:, last:], None, ALU.mult)
+        for c in range(2):
+            cols = slice(c * W, (c + 1) * W)
+            nc.vector.scalar_tensor_tensor(
+                z[:, cols, last], sent[last][:, cols], neg_gain[:], ub_gain[:, cols], ALU.mult, ALU.add)
         z_w = sb("z_w", [P, S], U32)
         z_s = sb("z_s", [P, S], U8)
         for c in range(2):

@@ -60,8 +60,8 @@ def tile_picked_dtzmthcpsdhaar_none_p_kernel(
         l_offs = load_list("offs", offs)
         xw = load_words(nc.sync, "xw", x_words, T)
         w1w = sb("w1w", [P, 2 * H], U8)
-        nc.scalar.dma_start(w1w[:].bitcast(I32), w1_words[0].bitcast(I32))
-        load_quadrant(nc.sync, w1s, w1_scales, 1)
+        load_quadrant(nc.scalar, w1s, w1_scales, 1)
+        nc.sync.dma_start(w1w[:].bitcast(I32), w1_words[0].bitcast(I32))
         load_quadrant(nc.sync, w1s, w1_scales, 2)
         l_n1 = load_list("n1", n1)
         l_n2 = load_list("n2", n2)
@@ -197,4 +197,5 @@ def tile_picked_dtzmthcpsdhaar_none_p_kernel(
             nc.scalar.activation(final[b][:].indirect(l_n6[:]), res2[b][:, 0, :], COPY, scale=0.75)
         for b in range(4):
             nc.scalar.activation(final[b][:].indirect(l_n7[:]), res2[b][:, 1, :], COPY)
-            nc.sync.dma_start(out[b * P:(b + 1) * P, :], final[b][:])
+            queue = nc.scalar if b == 3 else nc.sync
+            queue.dma_start(out[b * P:(b + 1) * P, :], final[b][:])

from contextlib import ExitStack

import concourse.mybir as mybir

F32 = mybir.dt.float32
BF16 = mybir.dt.bfloat16
I32 = mybir.dt.int32
U32 = mybir.dt.uint32
U16 = mybir.dt.uint16
U8 = mybir.dt.uint8
FP8X4 = mybir.dt.float8_e4m3fn_x4
FP4X4 = mybir.dt.float4_e2m1fn_x4
ALU = mybir.AluOpType
COPY = mybir.ActivationFunctionType.Copy

P = 128
PACK = 4
T, S, H, W, G = 1024, 256, 512, 128, 2048
FLOPS = 4 * 2 * 512 * H * S


def tile_picked_dtzmthcpsdhaar_none_p_kernel(
    tc, x_words, x_scales, w1_words, w1_scales, gs, d_words, d_scales,
    offs, n1, n2, n3, n4, n5, k1, k2, two, k3, hz, n6, n7, out,
):
    nc = tc.nc
    with ExitStack() as ctx:
        lists = ctx.enter_context(tc.tile_pool(name="lists", bufs=1))
        keep = ctx.enter_context(tc.tile_pool(name="keep", bufs=1))
        psum = ctx.enter_context(tc.psum_pool(name="psum", bufs=1))

        def sb(name, shape, dtype, tag=None):
            return keep.tile(shape, dtype, name=name, tag=tag or name, align_bytes=64)

        def load_list(name, src):
            tile = lists.tile(list(src.shape), U16, name="list_" + name)
            nc.sync.dma_start(tile[:], src)
            return tile

        def load_quadrant(queue, tile, src, q):
            rows = src[0].bitcast(I32)[4 * q:4 * q + 4, :]
            queue.dma_start(tile[32 * q:32 * q + 32, :].bitcast(I32), rows.partition_broadcast(8))

        def load_words(queue, name, src, cols):
            tile = sb(name, [P, cols], U32)
            queue.dma_start(tile[:].bitcast(I32), src[0].rearrange("p n t -> p (n t)").bitcast(I32))
            return tile

        def gather(dst, window, offsets):
            nc.vector.tensor_copy(dst, window[:].indirect(offsets[:]))

        xs = sb("xs", [P, T], U8)
        w1s = sb("w1s", [P, H], U8)
        load_quadrant(nc.gpsimd, w1s, w1_scales, 3)
        load_quadrant(nc.scalar, xs, x_scales, 0)
        load_quadrant(nc.sync, xs, x_scales, 3)
        load_quadrant(nc.scalar, xs, x_scales, 1)
        load_quadrant(nc.sync, xs, x_scales, 2)
        load_quadrant(nc.scalar, w1s, w1_scales, 0)
        l_offs = load_list("offs", offs)
        xw = load_words(nc.sync, "xw", x_words, T)
        w1w = sb("w1w", [P, 2 * H], U8)
        load_quadrant(nc.scalar, w1s, w1_scales, 1)
        nc.sync.dma_start(w1w[:].bitcast(I32), w1_words[0].bitcast(I32))
        load_quadrant(nc.sync, w1s, w1_scales, 2)
        l_n1 = load_list("n1", n1)
        l_n2 = load_list("n2", n2)
        l_n3 = load_list("n3", n3)
        l_n4 = load_list("n4", n4)
        dsc = sb("dsc", [P, G], U8)
        nc.vector.memset(dsc[:].bitcast(I32), 0)
        for r in range(4):
            first = r if r < 2 else 16 + r
            nc.sync.dma_start(dsc[first:P:32, :].bitcast(I32), d_scales[0].bitcast(I32)[r:16:4, :])
        l_k1 = load_list("k1", k1)
        l_k2 = load_list("k2", k2)
        l_k3 = load_list("k3", k3)
        l_hz = load_list("hz", hz)
        l_two = load_list("two", two)
        dw = load_words(nc.sync, "dw", d_words, G)
        l_n5 = load_list("n5", n5)
        gain = sb("gain", [P, PACK], F32)
        nc.sync.dma_start(gain[:], gs.rearrange("(p t) o -> p (t o)", t=PACK))
        l_n6 = load_list("n6", n6)
        l_n7 = load_list("n7", n7)

        xq_s = sb("xq_s", [P, S], U8)
        gather(xq_s[:], xs, l_offs)
        xq_w = sb("xq_w", [P, S], U32)
        for c in range(2):
            nc.vector.tensor_copy(xq_w[:, c * W:(c + 1) * W], xw[:].indirect(l_offs[:, c * W // 16:(c + 1) * W // 16]))
        groups = [(0, 0, W), (0, W, W)] + [(b, 0, S) for b in range(1, 4)]
        wc = [sb("wc%d" % t, [P, 2 * P], U8) for t in range(PACK)]
        ws = [sb("ws%d" % t, [P, P], U8) for t in range(PACK)]
        for t in range(PACK):
            nc.scalar.copy(wc[t][:].bitcast(U16), w1w[:].bitcast(U16)[:, t::PACK])
            nc.gpsimd.tensor_copy(ws[t][:], w1s[:, t::PACK])
        y = [sb("y%d" % t, [P, S], F32) for t in range(PACK)]
        for g, (t, c, n) in enumerate(groups):
            bank = psum.tile([P, n], F32, name="ybank%d" % g, tag="bank%d" % g)
            nc.tensor.matmul_mx(
                out=bank[:], lhsT=wc[t][:].bitcast(FP4X4), lhsT_scale=ws[t][:],
                rhs=xq_w[:, c:c + n].bitcast(FP8X4), rhs_scale=xq_s[:, c:c + n], start=True, stop=True,
            )
            if g == 0:
                nc.scalar.copy(y[t][:, c:c + n], bank[:])
            else:
                nc.vector.tensor_copy(y[t][:, c:c + n], bank[:])

        pa = [sb("pa%d" % t, [P, W], F32) for t in range(PACK)]
        pb = [sb("pb%d" % t, [P, W], F32) for t in range(PACK)]
        res = [sb("res%d" % t, [P, 2, W], F32) for t in range(PACK)]
        for t in range(PACK):
            nc.scalar.activation(pa[t][:], y[t][:].indirect(l_n1[:]), COPY)
            nc.scalar.activation(pb[t][:], y[t][:].indirect(l_n2[:]), COPY)
        for t in range(PACK):
            nc.vector.tensor_tensor(res[t][:, 0, :], pa[t][:], pb[t][:], ALU.min)
            nc.vector.tensor_tensor(res[t][:, 1, :], pa[t][:], pb[t][:], ALU.add)
        ub = [sb("ub%d" % t, [P, S], F32) for t in range(PACK)]
        sent = [sb("sent%d" % t, [P, 2 * S], F32) for t in range(PACK)]
        for first in (0, 2):
            for lst, side in ((l_n3, 0), (l_n4, 1)):
                for t in (first, first + 1):
                    nc.scalar.activation(ub[t][:].indirect(lst[:]), res[t][:, side, :], COPY)
        for t in range(PACK):
            nc.scalar.activation(sent[t][:].indirect(l_n5[:]), ub[t][:], COPY)

        picked = sb("picked", [P, 3 * H + 2 * S], U8, tag="pa1")
        words = sb("words", [P, 3 * H + 2 * S], U32, tag="pb3")
        moved = 3 * H + S
        for i, lst in enumerate((l_k1, l_k2, l_k3)):
            gather(picked[:, i * H:(i + 1) * H], dsc, lst)
        gather(picked[:, 3 * H:moved], xs, l_hz)
        placed = sb("placed", [P, moved], U8)
        nc.gpsimd.memset(placed[:].bitcast(I32), 0)
        for r in range(4):
            first = r if r < 2 else 16 + r
            nc.sync.dma_start(placed[r:P:32, :].bitcast(I32), picked[first:P:32, 0:moved].bitcast(I32))
        gather(picked[:, moved:], xs, l_two)
        gather(words[:, 3 * H:moved], xw, l_hz)
        gather(words[:, moved:], xw, l_two)
        for i, lst in ((1, l_k2), (2, l_k3), (0, l_k1)):
            gather(words[:, i * H:(i + 1) * H], dw, lst)

        hbank = [psum.tile([P, n], F32, name="hbank%d" % g, tag="bank%d" % (7 - g)) for g, (b, c, n) in enumerate(groups)]

        def product(g, i, rhs, rhs_scale, start, stop):
            b, c, n = groups[g]
            cols = slice(i * H + b * P, i * H + (b + 1) * P)
            nc.tensor.matmul_mx(
                out=hbank[g][:], lhsT=words[:, cols].bitcast(FP8X4), lhsT_scale=placed[:, cols],
                rhs=rhs[:, c:c + n].bitcast(FP8X4), rhs_scale=rhs_scale[:, c:c + n], start=start, stop=stop,
            )

        for g in range(len(groups)):
            product(g, 1, words[:, moved:], picked[:, moved:], True, False)
            product(g, 2, words[:, 3 * H:moved], placed[:, 3 * H:], False, False)

        z = sb("z", [P, S, PACK], BF16, tag="dw")
        last = PACK - 1
        for t in range(last):
            diff = sb("diff%d" % t, [P, S], F32, tag="dsc" if t == 0 else None)
            nc.vector.tensor_tensor(diff[:], ub[t][:], sent[t][:, 0:S], ALU.subtract)
            nc.vector.tensor_scalar(z[:, :, t], diff[:], gain[:, t:t + 1], None, ALU.mult)
        neg_gain = sb("neg_gain", [P, 1], F32)
        nc.vector.tensor_scalar(neg_gain[:], gain[:, last:], -1.0, None, ALU.mult)
        ub_gain = sb("ub_gain", [P, S], F32, tag="xw")
        nc.vector.tensor_scalar(ub_gain[:], ub[last][:], gain[:, last:], None, ALU.mult)
        for c in range(2):
            cols = slice(c * W, (c + 1) * W)
            nc.vector.scalar_tensor_tensor(
                z[:, cols, last], sent[last][:, cols], neg_gain[:], ub_gain[:, cols], ALU.mult, ALU.add)
        z_w = sb("z_w", [P, S], U32)
        z_s = sb("z_s", [P, S], U8)
        for c in range(2):
            cols = slice(c * W, (c + 1) * W)
            nc.vector.quantize_mx(
                out=z_w[:, cols].bitcast(FP8X4), scales=z_s[:, cols], in_=z[:, cols, :].rearrange("p j t -> p (j t)"))

        h2 = [sb("h2_%d" % b, [P, S], F32) for b in range(4)]
        for g, (b, c, n) in enumerate(groups):
            product(g, 0, z_w[:], z_s[:], False, True)
            if g == 0:
                nc.scalar.activation(h2[b][:, c:c + n], hbank[g][:], COPY, scale=0.0625)
            else:
                nc.vector.tensor_scalar(h2[b][:, c:c + n], hbank[g][:], 0.0625, None, ALU.mult)
        pairs2 = [sb("pairs2_%d" % b, [P, 2, W], F32) for b in range(4)]
        res2 = [sb("res2_%d" % b, [P, 2, W], F32) for b in range(4)]
        for b in range(4):
            nc.scalar.activation(pairs2[b][:, 0, :], h2[b][:].indirect(l_n6[:]), COPY)
            nc.scalar.activation(pairs2[b][:, 1, :], h2[b][:].indirect(l_n7[:]), COPY)
        for b in range(4):
            nc.vector.tensor_tensor(res2[b][:, 0, :], pairs2[b][:, 0, :], pairs2[b][:, 1, :], ALU.add)
            nc.vector.tensor_tensor(res2[b][:, 1, :], pairs2[b][:, 0, :], pairs2[b][:, 1, :], ALU.subtract)
        final = [sb("final%d" % b, [P, S], F32) for b in range(4)]
        for b in range(4):
            nc.scalar.activation(final[b][:].indirect(l_n6[:]), res2[b][:, 0, :], COPY, scale=0.75)
        for b in range(4):
            nc.scalar.activation(final[b][:].indirect(l_n7[:]), res2[b][:, 1, :], COPY)
            queue = nc.scalar if b == 3 else nc.sync
            queue.dma_start(out[b * P:(b + 1) * P, :], final[b][:])
